import numpy as np
import ml_dtypes


def mxq(x, axis, fmt="e4m3"):
    dtype, down = {"e4m3": (ml_dtypes.float8_e4m3fn, 7), "e5m2": (ml_dtypes.float8_e5m2, 14)}[fmt]
    v = np.moveaxis(np.asarray(x, np.float32).astype(ml_dtypes.bfloat16).astype(np.float64), axis, -1)
    blocks = v.reshape(v.shape[:-1] + (-1, 32))
    amax = np.abs(blocks).max(-1, keepdims=True)
    byte = np.maximum(np.where(amax > 0, np.frexp(amax)[1] - 1 + 127, 0) - down, 1)
    scale = np.exp2(byte - 127.0)
    codes = (blocks / scale).astype(np.float32).astype(dtype).astype(np.float64)
    return np.moveaxis((codes * scale).reshape(v.shape), -1, axis)


WIDE = False


def mx_kscale(k):
    if not WIDE:
        return np.ones(k)
    levels = np.array([10, -10, 5, -5, 0])
    if k % 512:
        return np.exp2(np.random.permutation(np.resize(levels, k // 32))).repeat(32)
    a = np.empty((k // 512, 16))
    for p in range(k // 512):
        a[p, :8] = np.random.permutation(np.resize(levels, 8))
        for g in range(8):
            far = levels[np.abs(levels - a[p, g]) >= 10]
            a[p, g + 8] = far[np.random.randint(len(far))]
    return np.exp2(a.ravel()).repeat(32)


def f64(x):
    return np.asarray(x).astype(np.float64)


def striped(idx):
    return np.tile(idx.reshape(-1, 16).T, (8, 1)).astype(np.uint16)


def unstriped(offs):
    return offs[:16].T.reshape(-1).astype(np.int64)


def striped8(idx):
    return np.concatenate([x.reshape(-1, 16).T for x in idx]).astype(np.uint16)


def runs(offs, k):
    lists = np.stack([offs[16 * r : 16 * r + 16].T.reshape(-1) for r in range(8)]).astype(np.int64)
    return lists[np.arange(k) % 512 // 64]


def pack_weight(w):
    k, n = w.shape
    w = f64(np.asarray(w, np.float32).astype(ml_dtypes.bfloat16)).reshape(k // 32, 32, n)
    amax = np.abs(w).max(1)
    byte = np.clip(np.where(amax > 0, np.frexp(amax)[1] - 1 + 127 - 7, 1), 1, 254)
    scaled = (w * np.exp2(127.0 - byte)[:, None, :]).reshape(k, n).astype(np.float32)
    words = np.ascontiguousarray(scaled.reshape(k // 512, 128, 4, n).transpose(0, 1, 3, 2)).astype(ml_dtypes.float8_e4m3fn).view(np.uint8)
    return words, np.ascontiguousarray(byte.astype(np.uint8).reshape(k // 512, 16, n))


def unpack_weight(words, scales):
    g, p, n, _ = words.shape
    vals = np.ascontiguousarray(words).view(ml_dtypes.float8_e4m3fn).astype(np.float64) * np.repeat(np.exp2(scales.astype(np.float64) - 127.0), 8, axis=1)[..., None]
    return vals.transpose(0, 1, 3, 2).reshape(g * 512, n)


def sigmoid(v):
    return 1.0 / (1.0 + np.exp(-np.maximum(v, -700.0)))


K, T, S, H, C, W = 512, 2048, 512, 512, 512, 256


def setup_inputs():
    n = np.random.standard_normal
    s = mx_kscale(K)[:, None]
    packed_xT = pack_weight(n((K, T)) * s)
    perm = np.stack([np.random.permutation(S) for _ in range(8)])
    return {
        "x_words": packed_xT[0],
        "x_scales": packed_xT[1],
        "w1": (n((K, H)) / np.sqrt(K) / s).astype(np.float32),
        "w2": (n((K, H)) / np.sqrt(K) / s).astype(np.float32),
        "gs": (np.random.uniform(0.5, 1.5, (K, 1)) / s).astype(np.float32),
        "offs": striped(np.random.permutation(T)[:S]),
        "two": striped(np.random.permutation(T)[:S]),
        "n1": striped8(np.stack([np.random.permutation(S) for _ in range(8)])),
        "n2": striped8(np.stack([np.random.permutation(S) for _ in range(8)])),
        "cand": striped(np.random.permutation(T)[:C]),
        "n3": striped8(perm[:, :W]),
        "n4": striped8(perm[:, W:]),
    }


def reference(x_words, x_scales, w1, w2, gs, offs, two, n1, n2, cand, n3, n4):
    x_cand = unpack_weight(x_words, x_scales)[:, unstriped(cand)]
    xq = unpack_weight(x_words, x_scales)[:, unstriped(offs)]
    y = mxq(f64(w1), 0, "e4m3").T @ xq
    x_two = unpack_weight(x_words, x_scales)[:, unstriped(two)]
    d = mxq(f64(w2), 0, "e4m3").T @ x_two
    z = f64(gs) * ((y + y[np.arange(H)[:, None], runs(n1, H)]) * (sigmoid(d + d[np.arange(H)[:, None], runs(n2, H)])))
    s = 0.0625 * ((x_cand.T @ mxq(z, 0, "e4m3")))
    pb = s[np.arange(C)[:, None], runs(n4, C)]
    pa = s[np.arange(C)[:, None], runs(n3, C)]
    rb = pb - (0.5 * pa)
    ra = np.sqrt((pa) ** 2 + (pb) ** 2 + 0.25)
    ds = np.zeros((C, S))
    ds[np.arange(C)[:, None], runs(n3, C)] = ra
    out = ds.copy()
    out[np.arange(C)[:, None], runs(n4, C)] = rb
    return out

@@ -1,0 +1,264 @@
+from contextlib import ExitStack
+
+import concourse.mybir as mybir
+from concourse.masks import make_identity
+
+K, T, S, H, C, W = 512, 2048, 512, 512, 512, 256
+FLOPS = 3 * 2 * 512 * 512 * 512
+
+F32 = mybir.dt.float32
+BF16 = mybir.dt.bfloat16
+I32 = mybir.dt.int32
+U32 = mybir.dt.uint32
+U16 = mybir.dt.uint16
+U8 = mybir.dt.uint8
+FP8X4 = mybir.dt.float8_e4m3fn_x4
+ACT = mybir.ActivationFunctionType
+ALU = mybir.AluOpType
+
+P = 128
+PACK = 4
+HALF = 256
+
+
+def tile_picked_twctriebpolar_none_p_kernel(
+    tc, x_words, x_scales, w1, w2, gs, offs, two, n1, n2, cand, n3, n4, out
+):
+    nc = tc.nc
+    with ExitStack() as ctx:
+        keep = ctx.enter_context(tc.tile_pool(name="keep", bufs=1))
+        psum = ctx.enter_context(tc.psum_pool(name="psum", bufs=1))
+
+        def sb(name, shape, dtype, tag=None):
+            return keep.tile(shape, dtype, name=name, tag=tag or name, align_bytes=64)
+
+        def bank(tag, name):
+            return psum.tile([P, 512], F32, name=name, tag=tag)
+
+        def load_list(name, src):
+            tile = keep.tile(list(src.shape), U16, name=name)
+            nc.sync.dma_start(tile[:], src)
+            return tile
+
+        def load_weight_half(name, w, h):
+            raw = sb(name, [P, PACK * HALF], F32)
+            nc.sync.dma_start(raw[:].rearrange("p (j c) -> p j c", j=PACK), w.rearrange("(p j) c -> p j c", j=PACK)[:, :, h * HALF : (h + 1) * HALF])
+            return raw
+
+        def cast_weight_half(grouped, raw, h):
+            m = HALF // PACK
+            nc.scalar.copy(
+                grouped[:].rearrange("p (t m j) -> p m j t", t=PACK, j=PACK)[:, h * m : (h + 1) * m],
+                raw[:].rearrange("p (j m t) -> p m j t", j=PACK, t=PACK),
+            )
+
+        def gather_packed(name, table, dtype, offsets, tag=None):
+            picked = sb(name, [P, S], dtype, tag)
+            nc.vector.tensor_copy(picked[:], table.indirect(offsets[:]))
+            return picked
+
+        def quantize(codes, scales, src, c0, c1):
+            nc.vector.quantize_mx(
+                out=codes[:, c0:c1].bitcast(FP8X4), scales=scales[:, c0:c1], in_=src[:, PACK * c0 : PACK * c1]
+            )
+
+        def product(acc, l_codes, l_scales, t, r_codes, r_scales, c0, c1):
+            nc.tensor.matmul_mx(
+                out=acc[:, c0:c1],
+                lhsT=l_codes[:, t * P : (t + 1) * P].bitcast(FP8X4),
+                lhsT_scale=l_scales[:, t * P : (t + 1) * P],
+                rhs=r_codes[:, c0:c1].bitcast(FP8X4),
+                rhs_scale=r_scales[:, c0:c1],
+                start=True,
+                stop=True,
+            )
+
+        def turn(dst, src, start, stop):
+            nc.tensor.matmul(dst, lhsT=src, rhs=ident[:], is_transpose=True, start=start, stop=stop)
+
+        def blk(i):
+            return slice(i * P, (i + 1) * P)
+
+        seen = {}
+        xs = sb("xs", [P, T], U8)
+        nc.gpsimd.memset(xs[:].bitcast(I32), 0)
+        two_l = load_list("two_l", two)
+        offs_l = load_list("offs_l", offs)
+        cand_l = load_list("cand_l", cand)
+        for q in range(4):
+            nc.sync.dma_start(xs[32 * q : 32 * q + 4, :].bitcast(I32), x_scales[0, 4 * q : 4 * q + 4, :].bitcast(I32))
+        xw = sb("xw", [P, T], I32)
+        nc.sync.dma_start(xw[:], x_words[0].rearrange("p n t -> p (n t)").bitcast(I32))
+        w2_raw = [load_weight_half("w2_raw0", w2, 0)]
+        w2_raw.append(load_weight_half("w2_raw1", w2, 1))
+        w1_raw = [load_weight_half("w1_raw%d" % h, w1, h) for h in range(2)]
+        n2_l = load_list("n2_l", n2)
+        gs_t = sb("gs_t", [P, PACK], F32)
+        nc.sync.dma_start(gs_t[:], gs.rearrange("(p t) o -> p (t o)", t=PACK))
+        n1_l = load_list("n1_l", n1)
+        n3_l = load_list("n3_l", n3)
+        n4_l = load_list("n4_l", n4)
+
+        ident = sb("ident", [P, P], F32)
+        make_identity(nc, ident[:])
+        warm = sb("warm", [P, 2], F32)
+        nc.scalar.activation(warm[:, 0:1], ident[:, 0:1], ACT.Sigmoid)
+
+        words = xw[:].bitcast(U32)
+        two_s = gather_packed("two_s", xs[:], U8, two_l)
+        offs_s = gather_packed("offs_s", xs[:], U8, offs_l)
+        cand_s = gather_packed("cand_s", xs[:], U8, cand_l)
+        two_w = gather_packed("two_w", words, U32, two_l)
+        offs_w = gather_packed("offs_w", words, U32, offs_l)
+
+        w2_g = sb("w2_g", [P, PACK * H], BF16)
+        for h in range(2):
+            cast_weight_half(w2_g, w2_raw[h], h)
+        w2_c = sb("w2_c", [P, H], U32)
+        w2_s = sb("w2_s", [P, H], U8)
+        quantize(w2_c, w2_s, w2_g, 0, H)
+
+        cand_w = gather_packed("cand_w", words, U32, cand_l, "w2_g")
+
+        def deal(name, picked, dtype, t0, t1, tag=None):
+            dealt = sb(name, [P, (t1 - t0) * P], dtype, tag)
+            nc.vector.tensor_copy(
+                dealt[:].rearrange("p (t m) -> p t m", m=P), picked[:].rearrange("p (m t) -> p t m", t=PACK)[:, t0:t1]
+            )
+            return dealt
+
+        cs = deal("cs", cand_s, U8, 0, PACK)
+        cw = deal("cw", cand_w, U32, 0, PACK)
+
+        w1_g = sb("w1_g", [P, PACK * H], BF16)
+        cast_weight_half(w1_g, w1_raw[0], 0)
+        rows = [w2_raw[0], w2_raw[1], w1_raw[1], w1_raw[0]]
+        for t in range(PACK):
+            acc = bank("a%d" % t, "d_acc%d" % t)
+            product(acc, w2_c, w2_s, t, two_w, two_s, 0, S)
+            nc.scalar.copy(rows[t][:, 0:S], acc[:])
+            if t == 1:
+                cast_weight_half(w1_g, w1_raw[1], 1)
+
+        def fetch(name, window, offsets, c0, c1, tag=None):
+            got = sb(name, [P, c1 - c0], F32, tag)
+            seen[name] = got
+            nc.vector.tensor_copy(got[:], window[:].indirect(offsets[:, c0 // 16 : c1 // 16]))
+            return got
+
+        d_sum = [bank("b%d" % jb, "d_sum%d" % jb) for jb in range(4)]
+        w1_c = sb("w1_c", [P, H], U32)
+        w1_s = sb("w1_s", [P, H], U8)
+        for t in range(PACK):
+            for jb in range(4):
+                turn(d_sum[jb][:, blk(t)], rows[t][:, blk(jb)], t == 0, False)
+            got = fetch("d_got%d" % t, rows[t], n2_l, 0, S, "w1_g" if t == 2 else None)
+            for jb in range(4):
+                turn(d_sum[jb][:, blk(t)], got[:, blk(jb)], False, t == PACK - 1)
+            if t == 1:
+                quantize(w1_c, w1_s, w1_g, 0, H)
+
+        for t in range(PACK):
+            acc = bank("a%d" % t, "y_acc%d" % t)
+            product(acc, w1_c, w1_s, t, offs_w, offs_s, 0, S)
+            nc.scalar.activation(rows[t][:, 0:S], acc[:], ACT.Copy, scale=gs_t[:, t : t + 1])
+
+        def upe(bank_tile):
+            return bank_tile[:].rearrange("j (u e p) -> j u p e", u=2, e=2)
+
+        gates = sb("gates", [P, 4 * H], F32, "gs_t")
+        gate = [gates[:, jb * H : (jb + 1) * H] for jb in range(4)]
+        for jb in range(4):
+            nc.scalar.activation(gate[jb].rearrange("j (u p e) -> j u p e", u=2, e=2), upe(d_sum[jb]), ACT.Sigmoid)
+        nc.scalar.activation(warm[:, 1:2], gate[3][:, 0:1], ACT.Sqrt)
+
+        y_sum = [bank("a%d" % jb, "y_sum%d" % jb) for jb in range(4)]
+        for t in range(PACK):
+            for jb in range(4):
+                turn(y_sum[jb][:, blk(t)], rows[t][:, blk(jb)], t == 0, False)
+            for c0, c1 in [(0, S)] if t < PACK - 1 else [(0, HALF), (HALF, S)]:
+                got = fetch("y_got%d_%d" % (t, c0), rows[t], n1_l, c0, c1)
+                for i in range((c1 - c0) // P):
+                    turn(y_sum[c0 // P + i][:, blk(t)], got[:, blk(i)], False, t == PACK - 1)
+
+        z_g = sb("z_g", [P, PACK * S], BF16)
+        z_c = sb("z_c", [P, S], U32)
+        z_s = sb("z_s", [P, S], U8)
+        for jb in range(4):
+            z_t = sb("z_t%d" % jb, [P, H], BF16)
+            seen["z_t%d" % jb] = z_t
+            nc.vector.tensor_tensor(
+                z_t[:].rearrange("j (u p e) -> j u p e", u=2, e=2),
+                upe(y_sum[jb]),
+                gate[jb].rearrange("j (u p e) -> j u p e", u=2, e=2),
+                ALU.mult,
+            )
+            z_w = bank("a%d" % jb, "z_w%d" % jb)
+            for u in range(2):
+                nc.tensor.transpose(z_w[:, blk(u)], z_t[:].bitcast(F32)[:, blk(u)], ident[:])
+            nc.scalar.copy(
+                z_g[:].bitcast(F32)[:, 2 * P * jb : 2 * P * (jb + 1)].rearrange("p (j u) -> p j u", u=2),
+                z_w[:, 0 : 2 * P].rearrange("p (u j) -> p j u", u=2),
+            )
+        pieces = [(0, 256), (256, 384), (384, 512)]
+        for c0, c1 in pieces:
+            quantize(z_c, z_s, z_g, c0, c1)
+
+        s_sb = []
+        for t in range(PACK):
+            acc = bank("b%d" % t, "s_acc%d" % t)
+            s_sb.append(sb("s_sb%d" % t, [P, S], F32))
+            if t == 0:
+                last = bank("a0", "s_last")
+                for c0, c1 in pieces[:2]:
+                    product(acc, cw, cs, t, z_c, z_s, c0, c1)
+                nc.scalar.activation(s_sb[t][:, 0:384], acc[:, 0:384], ACT.Copy, scale=0.0625)
+                product(last, cw, cs, t, z_c, z_s, 384, 512)
+                nc.scalar.activation(s_sb[t][:, 384:512], last[:, 384:512], ACT.Copy, scale=0.0625)
+            else:
+                for c0, c1 in pieces:
+                    product(acc, cw, cs, t, z_c, z_s, c0, c1)
+                nc.scalar.activation(s_sb[t][:], acc[:], ACT.Copy, scale=0.0625)
+
+        out_rows = out.rearrange("(p t) s -> t p s", t=PACK)
+        half_a, pb, ra, res = {}, {}, {}, {}
+
+        def pairs(t):
+            half_a[t] = sb("half_a%d" % t, [P, W], F32)
+            pb[t] = sb("pb%d" % t, [P, W], F32)
+            nc.vector.tensor_scalar(half_a[t][:], s_sb[t][:].indirect(n3_l[:]), -0.5, 0.0, ALU.mult, ALU.add)
+            nc.vector.tensor_copy(pb[t][:], s_sb[t][:].indirect(n4_l[:]))
+            turned = bank("a%d" % (2 * (t % 2)), "turned%d" % t)
+            for i in range(2):
+                nc.tensor.transpose(turned[:, blk(i)], half_a[t][:, blk(i)], ident[:])
+                nc.tensor.transpose(turned[:, blk(2 + i)], pb[t][:, blk(i)], ident[:])
+            sq = sb("sq%d" % t, [P, 2 * W], F32)
+            nc.scalar.activation(sq[:, 0:W], turned[:, 0:W], ACT.Square, scale=2.0)
+            nc.scalar.activation(sq[:, W : 2 * W], turned[:, W : 2 * W], ACT.Square)
+            total = bank("a%d" % (2 * (t % 2) + 1), "total%d" % t)
+            for i in range(2):
+                turn(total[:, blk(i)], sq[:, blk(i)], True, False)
+                turn(total[:, blk(i)], sq[:, blk(2 + i)], False, True)
+            ra[t] = sb("ra%d" % t, [P, W], F32)
+            nc.scalar.activation(ra[t][:], total[:, 0:W], ACT.Sqrt, bias=0.25)
+
+        def put_rb(t):
+            res[t] = sb("res%d" % t, [P, S], F32)
+            nc.vector.tensor_tensor(res[t][:].indirect(n4_l[:]), pb[t][:], half_a[t][:], ALU.add)
+
+        def put_ra(t):
+            nc.vector.tensor_copy(res[t][:].indirect(n3_l[:]), ra[t][:])
+            nc.sync.dma_start(out_rows[t], res[t][:])
+
+        pairs(0)
+        pairs(1)
+        put_rb(0)
+        put_rb(1)
+        put_ra(0)
+        pairs(2)
+        put_ra(1)
+        pairs(3)
+        put_rb(2)
+        put_rb(3)
+        put_ra(2)
+        put_ra(3)

@@ -59,7 +59,7 @@ def tile_picked_twctriebpolar_none_p_kernel(
 
         def quantize(codes, scales, src, c0, c1):
             nc.vector.quantize_mx(
-                out=codes[:, c0:c1].bitcast(FP8X4), scales=scales[:, c0:c1], in_=src[:, PACK * c0 : PACK * c1]
+                out=codes[:, c0:c1].bitcast(FP8X4), scales=scales[:, c0:c1], in_=src
             )
 
         def product(acc, l_codes, l_scales, t, r_codes, r_scales, c0, c1):
@@ -87,10 +87,9 @@ def tile_picked_twctriebpolar_none_p_kernel(
         cand_l = load_list("cand_l", cand)
         for q in range(4):
             nc.sync.dma_start(xs[32 * q : 32 * q + 4, :].bitcast(I32), x_scales[0, 4 * q : 4 * q + 4, :].bitcast(I32))
+        w2_raw = [load_weight_half("w2_raw%d" % h, w2, h) for h in range(2)]
         xw = sb("xw", [P, T], I32)
         nc.sync.dma_start(xw[:], x_words[0].rearrange("p n t -> p (n t)").bitcast(I32))
-        w2_raw = [load_weight_half("w2_raw0", w2, 0)]
-        w2_raw.append(load_weight_half("w2_raw1", w2, 1))
         w1_raw = [load_weight_half("w1_raw%d" % h, w1, h) for h in range(2)]
         n2_l = load_list("n2_l", n2)
         gs_t = sb("gs_t", [P, PACK], F32)
@@ -101,34 +100,35 @@ def tile_picked_twctriebpolar_none_p_kernel(
 
         ident = sb("ident", [P, P], F32)
         make_identity(nc, ident[:])
-        warm = sb("warm", [P, 2], F32)
-        nc.scalar.activation(warm[:, 0:1], ident[:, 0:1], ACT.Sigmoid)
+        warm = sb("warm", [P, 3], F32)
+        nc.vector.memset(warm[:, 2:3], 0.0)
+        nc.scalar.activation(warm[:, 0:1], warm[:, 2:3], ACT.Sigmoid)
 
         words = xw[:].bitcast(U32)
         two_s = gather_packed("two_s", xs[:], U8, two_l)
         offs_s = gather_packed("offs_s", xs[:], U8, offs_l)
         cand_s = gather_packed("cand_s", xs[:], U8, cand_l)
-        two_w = gather_packed("two_w", words, U32, two_l)
-        offs_w = gather_packed("offs_w", words, U32, offs_l)
 
         w2_g = sb("w2_g", [P, PACK * H], BF16)
         for h in range(2):
             cast_weight_half(w2_g, w2_raw[h], h)
         w2_c = sb("w2_c", [P, H], U32)
         w2_s = sb("w2_s", [P, H], U8)
-        quantize(w2_c, w2_s, w2_g, 0, H)
+        quantize(w2_c, w2_s, w2_g[:], 0, H)
 
-        cand_w = gather_packed("cand_w", words, U32, cand_l, "w2_g")
+        two_w = gather_packed("two_w", words, U32, two_l)
+        offs_w = gather_packed("offs_w", words, U32, offs_l)
+        cand_w = gather_packed("cand_w", words, U32, cand_l)
 
         def deal(name, picked, dtype, t0, t1, tag=None):
             dealt = sb(name, [P, (t1 - t0) * P], dtype, tag)
             nc.vector.tensor_copy(
-                dealt[:].rearrange("p (t m) -> p t m", m=P), picked[:].rearrange("p (m t) -> p t m", t=PACK)[:, t0:t1]
+                dealt[:].rearrange("p (t m) -> p m t", m=P), picked[:].rearrange("p (m t) -> p m t", t=PACK)[:, :, t0:t1]
             )
             return dealt
 
-        cs = deal("cs", cand_s, U8, 0, PACK)
-        cw = deal("cw", cand_w, U32, 0, PACK)
+        cs = deal("cs", cand_s, U8, 0, 1)
+        cw = deal("cw", cand_w, U32, 0, 1)
 
         w1_g = sb("w1_g", [P, PACK * H], BF16)
         cast_weight_half(w1_g, w1_raw[0], 0)
@@ -146,79 +146,102 @@ def tile_picked_twctriebpolar_none_p_kernel(
             nc.vector.tensor_copy(got[:], window[:].indirect(offsets[:, c0 // 16 : c1 // 16]))
             return got
 
-        d_sum = [bank("b%d" % jb, "d_sum%d" % jb) for jb in range(4)]
+        def place(sums, t, jb):
+            c0 = (jb % 2) * 2 * P + (t % 2) * P
+            return sums[2 * (t // 2) + jb // 2][:, c0 : c0 + P]
+
+        def turn_own(sums, t):
+            for jb in range(4):
+                turn(place(sums, t, jb), rows[t][:, blk(jb)], t % 2 == 0 and jb % 2 == 0, False)
+
+        def turn_fetched(sums, t, got, c0, c1):
+            for jb in range(c0 // P, c1 // P):
+                turn(place(sums, t, jb), got[:, blk(jb - c0 // P)], False, t % 2 == 1 and jb % 2 == 1)
+
+        def ipe(bank_tile):
+            return bank_tile[:].rearrange("j (i e p) -> j i p e", i=2, e=2)
+
+        d_sum = [bank("b%d" % n, "d_sum%d" % n) for n in range(4)]
         w1_c = sb("w1_c", [P, H], U32)
         w1_s = sb("w1_s", [P, H], U8)
         for t in range(PACK):
-            for jb in range(4):
-                turn(d_sum[jb][:, blk(t)], rows[t][:, blk(jb)], t == 0, False)
+            turn_own(d_sum, t)
             got = fetch("d_got%d" % t, rows[t], n2_l, 0, S, "w1_g" if t == 2 else None)
-            for jb in range(4):
-                turn(d_sum[jb][:, blk(t)], got[:, blk(jb)], False, t == PACK - 1)
+            turn_fetched(d_sum, t, got, 0, S)
             if t == 1:
-                quantize(w1_c, w1_s, w1_g, 0, H)
+                quantize(w1_c, w1_s, w1_g[:], 0, H)
 
+        gate = []
+
+        def make_gates(u, tag):
+            both = sb("gates%d" % u, [P, 2 * H], F32, tag)
+            for h in range(2):
+                gate.append(both[:, h * H : (h + 1) * H].rearrange("j (i p e) -> j i p e", i=2, e=2))
+                nc.scalar.activation(gate[-1], ipe(d_sum[2 * u + h]), ACT.Sigmoid)
+            return both
+
+        make_gates(0, None)
         for t in range(PACK):
             acc = bank("a%d" % t, "y_acc%d" % t)
             product(acc, w1_c, w1_s, t, offs_w, offs_s, 0, S)
             nc.scalar.activation(rows[t][:, 0:S], acc[:], ACT.Copy, scale=gs_t[:, t : t + 1])
 
-        def upe(bank_tile):
-            return bank_tile[:].rearrange("j (u e p) -> j u p e", u=2, e=2)
+        late = make_gates(1, "gs_t")
+        nc.scalar.activation(warm[:, 1:2], late[:, H : H + 1], ACT.Sqrt)
 
-        gates = sb("gates", [P, 4 * H], F32, "gs_t")
-        gate = [gates[:, jb * H : (jb + 1) * H] for jb in range(4)]
-        for jb in range(4):
-            nc.scalar.activation(gate[jb].rearrange("j (u p e) -> j u p e", u=2, e=2), upe(d_sum[jb]), ACT.Sigmoid)
-        nc.scalar.activation(warm[:, 1:2], gate[3][:, 0:1], ACT.Sqrt)
+        y_sum = [bank("a%d" % n, "y_sum%d" % n) for n in range(4)]
+        z_first = sb("z_first", [P, 2 * H], BF16, "w1_raw1")
+        z_t = [z_first[:, 0:H], z_first[:, H : 2 * H]] + [sb("z_t%d" % n, [P, H], BF16)[:] for n in (2, 3)]
+        z_w = [bank("b%d" % jb, "z_w%d" % jb) for jb in range(4)]
 
-        y_sum = [bank("a%d" % jb, "y_sum%d" % jb) for jb in range(4)]
+        def gated(n):
+            nc.vector.tensor_tensor(
+                z_t[n].rearrange("j (i p e) -> j i p e", i=2, e=2), ipe(y_sum[n]), gate[n], ALU.mult
+            )
+
+        def turn_back(n):
+            for i in range(2):
+                nc.tensor.transpose(z_w[2 * (n % 2) + i][:, blk(n // 2)], z_t[n].bitcast(F32)[:, blk(i)], ident[:])
+
         for t in range(PACK):
-            for jb in range(4):
-                turn(y_sum[jb][:, blk(t)], rows[t][:, blk(jb)], t == 0, False)
+            turn_own(y_sum, t)
             for c0, c1 in [(0, S)] if t < PACK - 1 else [(0, HALF), (HALF, S)]:
                 got = fetch("y_got%d_%d" % (t, c0), rows[t], n1_l, c0, c1)
-                for i in range((c1 - c0) // P):
-                    turn(y_sum[c0 // P + i][:, blk(t)], got[:, blk(i)], False, t == PACK - 1)
+                turn_fetched(y_sum, t, got, c0, c1)
+            if t == 2:
+                gated(0)
+                gated(1)
+        for n in range(4):
+            if n >= 2:
+                gated(n)
+            turn_back(n)
 
-        z_g = sb("z_g", [P, PACK * S], BF16)
+        pieces = [(0, 256), (256, 384), (384, 512)]
         z_c = sb("z_c", [P, S], U32)
         z_s = sb("z_s", [P, S], U8)
-        for jb in range(4):
-            z_t = sb("z_t%d" % jb, [P, H], BF16)
-            seen["z_t%d" % jb] = z_t
-            nc.vector.tensor_tensor(
-                z_t[:].rearrange("j (u p e) -> j u p e", u=2, e=2),
-                upe(y_sum[jb]),
-                gate[jb].rearrange("j (u p e) -> j u p e", u=2, e=2),
-                ALU.mult,
-            )
-            z_w = bank("a%d" % jb, "z_w%d" % jb)
-            for u in range(2):
-                nc.tensor.transpose(z_w[:, blk(u)], z_t[:].bitcast(F32)[:, blk(u)], ident[:])
-            nc.scalar.copy(
-                z_g[:].bitcast(F32)[:, 2 * P * jb : 2 * P * (jb + 1)].rearrange("p (j u) -> p j u", u=2),
-                z_w[:, 0 : 2 * P].rearrange("p (u j) -> p j u", u=2),
-            )
-        pieces = [(0, 256), (256, 384), (384, 512)]
         for c0, c1 in pieces:
-            quantize(z_c, z_s, z_g, c0, c1)
+            z_g = sb("z_g%d" % c0, [P, PACK * (c1 - c0)], BF16)
+            for jb in range(c0 // P, c1 // P):
+                nc.scalar.copy(
+                    z_g[:].bitcast(F32)[:, 2 * (P * jb - c0) : 2 * (P * (jb + 1) - c0)].rearrange("p (j u) -> p j u", u=2),
+                    z_w[jb][:, 0 : 2 * P].rearrange("p (u j) -> p j u", u=2),
+                )
+            quantize(z_c, z_s, z_g[:], c0, c1)
 
-        s_sb = []
-        for t in range(PACK):
-            acc = bank("b%d" % t, "s_acc%d" % t)
-            s_sb.append(sb("s_sb%d" % t, [P, S], F32))
-            if t == 0:
-                last = bank("a0", "s_last")
-                for c0, c1 in pieces[:2]:
-                    product(acc, cw, cs, t, z_c, z_s, c0, c1)
-                nc.scalar.activation(s_sb[t][:, 0:384], acc[:, 0:384], ACT.Copy, scale=0.0625)
-                product(last, cw, cs, t, z_c, z_s, 384, 512)
-                nc.scalar.activation(s_sb[t][:, 384:512], last[:, 384:512], ACT.Copy, scale=0.0625)
-            else:
-                for c0, c1 in pieces:
-                    product(acc, cw, cs, t, z_c, z_s, c0, c1)
-                nc.scalar.activation(s_sb[t][:], acc[:], ACT.Copy, scale=0.0625)
+        s_sb = [sb("s_sb%d" % t, [P, S], F32) for t in range(PACK)]
+        acc = bank("a0", "s_acc0")
+        last = bank("a1", "s_last")
+        for c0, c1 in pieces[:2]:
+            product(acc, cw, cs, 0, z_c, z_s, c0, c1)
+        nc.scalar.activation(s_sb[0][:, 0:384], acc[:, 0:384], ACT.Copy, scale=0.0625)
+        product(last, cw, cs, 0, z_c, z_s, 384, 512)
+        nc.scalar.activation(s_sb[0][:, 384:512], last[:, 384:512], ACT.Copy, scale=0.0625)
+        cs_rest = deal("cs_rest", cand_s, U8, 1, PACK, "z_g256")
+        cw_rest = deal("cw_rest", cand_w, U32, 1, PACK, "z_g384")
+        for t in range(1, PACK):
+            acc = bank(["a2", "a3", "b0"][t - 1], "s_acc%d" % t)
+            product(acc, cw_rest, cs_rest, t - 1, z_c, z_s, 0, S)
+            nc.scalar.activation(s_sb[t][:], acc[:], ACT.Copy, scale=0.0625)
 
         out_rows = out.rearrange("(p t) s -> t p s", t=PACK)
         half_a, pb, ra, res = {}, {}, {}, {}
@@ -228,14 +251,14 @@ def tile_picked_twctriebpolar_none_p_kernel(
             pb[t] = sb("pb%d" % t, [P, W], F32)
             nc.vector.tensor_scalar(half_a[t][:], s_sb[t][:].indirect(n3_l[:]), -0.5, 0.0, ALU.mult, ALU.add)
             nc.vector.tensor_copy(pb[t][:], s_sb[t][:].indirect(n4_l[:]))
-            turned = bank("a%d" % (2 * (t % 2)), "turned%d" % t)
+            turned = bank(["b1", "b3"][t % 2], "turned%d" % t)
             for i in range(2):
                 nc.tensor.transpose(turned[:, blk(i)], half_a[t][:, blk(i)], ident[:])
                 nc.tensor.transpose(turned[:, blk(2 + i)], pb[t][:, blk(i)], ident[:])
             sq = sb("sq%d" % t, [P, 2 * W], F32)
             nc.scalar.activation(sq[:, 0:W], turned[:, 0:W], ACT.Square, scale=2.0)
             nc.scalar.activation(sq[:, W : 2 * W], turned[:, W : 2 * W], ACT.Square)
-            total = bank("a%d" % (2 * (t % 2) + 1), "total%d" % t)
+            total = bank(["b2", "a1"][t % 2], "total%d" % t)
             for i in range(2):
                 turn(total[:, blk(i)], sq[:, blk(i)], True, False)
                 turn(total[:, blk(i)], sq[:, blk(2 + i)], False, True)

@@ -3,7 +3,7 @@ from contextlib import ExitStack
 import concourse.mybir as mybir
 from concourse.masks import make_identity
 
-K, T, S, H, C, W = 512, 2048, 512, 512, 512, 256
+T, S, H, C, W = 2048, 512, 512, 512, 256
 FLOPS = 3 * 2 * 512 * 512 * 512
 
 F32 = mybir.dt.float32
@@ -19,6 +19,9 @@ ALU = mybir.AluOpType
 P = 128
 PACK = 4
 HALF = 256
+PER_COLUMN = 16
+SCORE_SCALE = 0.0625
+Z_PIECES = [(0, 256), (256, 384), (384, 512)]
 
 
 def tile_picked_twctriebpolar_none_p_kernel(
@@ -35,6 +38,9 @@ def tile_picked_twctriebpolar_none_p_kernel(
         def bank(tag, name):
             return psum.tile([P, 512], F32, name=name, tag=tag)
 
+        def blk(i):
+            return slice(i * P, (i + 1) * P)
+
         def load_list(name, src):
             tile = keep.tile(list(src.shape), U16, name=name)
             nc.sync.dma_start(tile[:], src)
@@ -42,7 +48,10 @@ def tile_picked_twctriebpolar_none_p_kernel(
 
         def load_weight_half(name, w, h):
             raw = sb(name, [P, PACK * HALF], F32)
-            nc.sync.dma_start(raw[:].rearrange("p (j c) -> p j c", j=PACK), w.rearrange("(p j) c -> p j c", j=PACK)[:, :, h * HALF : (h + 1) * HALF])
+            nc.sync.dma_start(
+                raw[:].rearrange("p (j c) -> p j c", j=PACK),
+                w.rearrange("(p j) c -> p j c", j=PACK)[:, :, h * HALF : (h + 1) * HALF],
+            )
             return raw
 
         def cast_weight_half(grouped, raw, h):
@@ -52,21 +61,25 @@ def tile_picked_twctriebpolar_none_p_kernel(
                 raw[:].rearrange("p (j m t) -> p m j t", j=PACK, t=PACK),
             )
 
-        def gather_packed(name, table, dtype, offsets, tag=None):
-            picked = sb(name, [P, S], dtype, tag)
-            nc.vector.tensor_copy(picked[:], table.indirect(offsets[:]))
+        def gather_packed(picked, table, offsets):
+            nc.vector.tensor_copy(picked, table.indirect(offsets[:]))
             return picked
 
-        def quantize(codes, scales, src, c0, c1):
-            nc.vector.quantize_mx(
-                out=codes[:, c0:c1].bitcast(FP8X4), scales=scales[:, c0:c1], in_=src
+        def deal(name, picked, dtype, t0, t1, tag=None):
+            dealt = sb(name, [P, (t1 - t0) * P], dtype, tag)
+            nc.vector.tensor_copy(
+                dealt[:].rearrange("p (t m) -> p m t", m=P), picked.rearrange("p (m t) -> p m t", t=PACK)[:, :, t0:t1]
             )
+            return dealt
+
+        def quantize(codes, scales, src, c0, c1):
+            nc.vector.quantize_mx(out=codes[:, c0:c1].bitcast(FP8X4), scales=scales[:, c0:c1], in_=src)
 
         def product(acc, l_codes, l_scales, t, r_codes, r_scales, c0, c1):
             nc.tensor.matmul_mx(
                 out=acc[:, c0:c1],
-                lhsT=l_codes[:, t * P : (t + 1) * P].bitcast(FP8X4),
-                lhsT_scale=l_scales[:, t * P : (t + 1) * P],
+                lhsT=l_codes[:, blk(t)].bitcast(FP8X4),
+                lhsT_scale=l_scales[:, blk(t)],
                 rhs=r_codes[:, c0:c1].bitcast(FP8X4),
                 rhs_scale=r_scales[:, c0:c1],
                 start=True,
@@ -76,10 +89,9 @@ def tile_picked_twctriebpolar_none_p_kernel(
         def turn(dst, src, start, stop):
             nc.tensor.matmul(dst, lhsT=src, rhs=ident[:], is_transpose=True, start=start, stop=stop)
 
-        def blk(i):
-            return slice(i * P, (i + 1) * P)
+        def fetch(got, window, offsets, c0, c1):
+            nc.vector.tensor_copy(got, window[:].indirect(offsets[:, c0 // PER_COLUMN : c1 // PER_COLUMN]))
 
-        seen = {}
         xs = sb("xs", [P, T], U8)
         nc.gpsimd.memset(xs[:].bitcast(I32), 0)
         two_l = load_list("two_l", two)
@@ -87,9 +99,9 @@ def tile_picked_twctriebpolar_none_p_kernel(
         cand_l = load_list("cand_l", cand)
         for q in range(4):
             nc.sync.dma_start(xs[32 * q : 32 * q + 4, :].bitcast(I32), x_scales[0, 4 * q : 4 * q + 4, :].bitcast(I32))
-        w2_raw = [load_weight_half("w2_raw%d" % h, w2, h) for h in range(2)]
         xw = sb("xw", [P, T], I32)
         nc.sync.dma_start(xw[:], x_words[0].rearrange("p n t -> p (n t)").bitcast(I32))
+        w2_raw = [load_weight_half("w2_raw%d" % h, w2, h) for h in range(2)]
         w1_raw = [load_weight_half("w1_raw%d" % h, w1, h) for h in range(2)]
         n2_l = load_list("n2_l", n2)
         gs_t = sb("gs_t", [P, PACK], F32)
@@ -100,14 +112,14 @@ def tile_picked_twctriebpolar_none_p_kernel(
 
         ident = sb("ident", [P, P], F32)
         make_identity(nc, ident[:])
-        warm = sb("warm", [P, 3], F32)
-        nc.vector.memset(warm[:, 2:3], 0.0)
-        nc.scalar.activation(warm[:, 0:1], warm[:, 2:3], ACT.Sigmoid)
 
         words = xw[:].bitcast(U32)
-        two_s = gather_packed("two_s", xs[:], U8, two_l)
-        offs_s = gather_packed("offs_s", xs[:], U8, offs_l)
-        cand_s = gather_packed("cand_s", xs[:], U8, cand_l)
+        picked_s = sb("picked_s", [P, 3 * S], U8)
+        two_s, offs_s, cand_s = [
+            gather_packed(picked_s[:, n * S : (n + 1) * S], xs[:], lst) for n, lst in enumerate((two_l, offs_l, cand_l))
+        ]
+        two_w = gather_packed(sb("two_w", [P, S], U32)[:], words, two_l)
+        offs_w = gather_packed(sb("offs_w", [P, S], U32)[:], words, offs_l)
 
         w2_g = sb("w2_g", [P, PACK * H], BF16)
         for h in range(2):
@@ -116,110 +128,91 @@ def tile_picked_twctriebpolar_none_p_kernel(
         w2_s = sb("w2_s", [P, H], U8)
         quantize(w2_c, w2_s, w2_g[:], 0, H)
 
-        two_w = gather_packed("two_w", words, U32, two_l)
-        offs_w = gather_packed("offs_w", words, U32, offs_l)
-        cand_w = gather_packed("cand_w", words, U32, cand_l)
-
-        def deal(name, picked, dtype, t0, t1, tag=None):
-            dealt = sb(name, [P, (t1 - t0) * P], dtype, tag)
-            nc.vector.tensor_copy(
-                dealt[:].rearrange("p (t m) -> p m t", m=P), picked[:].rearrange("p (m t) -> p m t", t=PACK)[:, :, t0:t1]
-            )
-            return dealt
-
+        cand_w = gather_packed(sb("cand_w", [P, C], U32, "w2_g")[:], words, cand_l)
         cs = deal("cs", cand_s, U8, 0, 1)
         cw = deal("cw", cand_w, U32, 0, 1)
 
         w1_g = sb("w1_g", [P, PACK * H], BF16)
         cast_weight_half(w1_g, w1_raw[0], 0)
-        rows = [w2_raw[0], w2_raw[1], w1_raw[1], w1_raw[0]]
+        d_rows = [w2_raw[0], w2_raw[1], w1_raw[1], w1_raw[0]]
         for t in range(PACK):
             acc = bank("a%d" % t, "d_acc%d" % t)
             product(acc, w2_c, w2_s, t, two_w, two_s, 0, S)
-            nc.scalar.copy(rows[t][:, 0:S], acc[:])
+            nc.scalar.copy(d_rows[t][:, 0:S], acc[:])
             if t == 1:
                 cast_weight_half(w1_g, w1_raw[1], 1)
-
-        def fetch(name, window, offsets, c0, c1, tag=None):
-            got = sb(name, [P, c1 - c0], F32, tag)
-            seen[name] = got
-            nc.vector.tensor_copy(got[:], window[:].indirect(offsets[:, c0 // 16 : c1 // 16]))
-            return got
 
         def place(sums, t, jb):
             c0 = (jb % 2) * 2 * P + (t % 2) * P
             return sums[2 * (t // 2) + jb // 2][:, c0 : c0 + P]
 
-        def turn_own(sums, t):
-            for jb in range(4):
-                turn(place(sums, t, jb), rows[t][:, blk(jb)], t % 2 == 0 and jb % 2 == 0, False)
+        def turn_own(sums, t, own):
+            for jb in range(PACK):
+                turn(place(sums, t, jb), own[:, blk(jb)], t % 2 == 0 and jb % 2 == 0, False)
 
         def turn_fetched(sums, t, got, c0, c1):
             for jb in range(c0 // P, c1 // P):
                 turn(place(sums, t, jb), got[:, blk(jb - c0 // P)], False, t % 2 == 1 and jb % 2 == 1)
 
-        def ipe(bank_tile):
+        def paired(bank_tile):
             return bank_tile[:].rearrange("j (i e p) -> j i p e", i=2, e=2)
 
-        d_sum = [bank("b%d" % n, "d_sum%d" % n) for n in range(4)]
-        w1_c = sb("w1_c", [P, H], U32)
-        w1_s = sb("w1_s", [P, H], U8)
+        def as_pairs(ap):
+            return ap.rearrange("j (i p e) -> j i p e", i=2, e=2)
+
+        d_sum = [bank("b%d" % n, "d_sum%d" % n) for n in range(PACK)]
+        y_rows, y_acc = [], []
         for t in range(PACK):
-            turn_own(d_sum, t)
-            got = fetch("d_got%d" % t, rows[t], n2_l, 0, S, "w1_g" if t == 2 else None)
-            turn_fetched(d_sum, t, got, 0, S)
+            turn_own(d_sum, t, d_rows[t])
+            y_rows.append(sb("y_rows%d" % t, [P, 2 * S], F32, "w1_g" if t == 2 else None))
+            fetch(y_rows[t][:, S : 2 * S], d_rows[t], n2_l, 0, S)
+            turn_fetched(d_sum, t, y_rows[t][:, S : 2 * S], 0, S)
             if t == 1:
+                w1_c = sb("w1_c", [P, H], U32)
+                w1_s = sb("w1_s", [P, H], U8)
                 quantize(w1_c, w1_s, w1_g[:], 0, H)
+                for n in range(PACK):
+                    y_acc.append(bank("a%d" % n, "y_acc%d" % n))
+                    product(y_acc[n], w1_c, w1_s, n, offs_w, offs_s, 0, S)
 
-        gate = []
-
-        def make_gates(u, tag):
-            both = sb("gates%d" % u, [P, 2 * H], F32, tag)
-            for h in range(2):
-                gate.append(both[:, h * H : (h + 1) * H].rearrange("j (i p e) -> j i p e", i=2, e=2))
-                nc.scalar.activation(gate[-1], ipe(d_sum[2 * u + h]), ACT.Sigmoid)
-            return both
-
-        make_gates(0, None)
         for t in range(PACK):
-            acc = bank("a%d" % t, "y_acc%d" % t)
-            product(acc, w1_c, w1_s, t, offs_w, offs_s, 0, S)
-            nc.scalar.activation(rows[t][:, 0:S], acc[:], ACT.Copy, scale=gs_t[:, t : t + 1])
+            nc.scalar.activation(y_rows[t][:, 0:S], y_acc[t][:], ACT.Copy, scale=gs_t[:, t : t + 1])
 
-        late = make_gates(1, "gs_t")
-        nc.scalar.activation(warm[:, 1:2], late[:, H : H + 1], ACT.Sqrt)
+        gates = sb("gates", [P, PACK * H], F32, "gs_t")
+        gate = [as_pairs(gates[:, n * H : (n + 1) * H]) for n in range(PACK)]
+        for n in range(PACK):
+            nc.scalar.activation(gate[n], paired(d_sum[n]), ACT.Sigmoid)
 
-        y_sum = [bank("a%d" % n, "y_sum%d" % n) for n in range(4)]
-        z_first = sb("z_first", [P, 2 * H], BF16, "w1_raw1")
+        y_sum = [bank("a%d" % n, "y_sum%d" % n) for n in range(PACK)]
+        for t in range(PACK):
+            turn_own(y_sum, t, y_rows[t])
+            for c0, c1 in [(0, S)] if t < PACK - 1 else [(0, HALF), (HALF, S)]:
+                got = sb("y_got%d_%d" % (t, c0), [P, c1 - c0], F32)
+                fetch(got[:], y_rows[t], n1_l, c0, c1)
+                turn_fetched(y_sum, t, got, c0, c1)
+
+        z_first = sb("z_first", [P, 2 * H], BF16, "w1_g")
         z_t = [z_first[:, 0:H], z_first[:, H : 2 * H]] + [sb("z_t%d" % n, [P, H], BF16)[:] for n in (2, 3)]
-        z_w = [bank("b%d" % jb, "z_w%d" % jb) for jb in range(4)]
+        z_w = [bank("b%d" % jb, "z_w%d" % jb) for jb in range(PACK)]
 
         def gated(n):
-            nc.vector.tensor_tensor(
-                z_t[n].rearrange("j (i p e) -> j i p e", i=2, e=2), ipe(y_sum[n]), gate[n], ALU.mult
-            )
+            nc.vector.tensor_tensor(as_pairs(z_t[n]), paired(y_sum[n]), gate[n], ALU.mult)
 
         def turn_back(n):
             for i in range(2):
                 nc.tensor.transpose(z_w[2 * (n % 2) + i][:, blk(n // 2)], z_t[n].bitcast(F32)[:, blk(i)], ident[:])
 
-        for t in range(PACK):
-            turn_own(y_sum, t)
-            for c0, c1 in [(0, S)] if t < PACK - 1 else [(0, HALF), (HALF, S)]:
-                got = fetch("y_got%d_%d" % (t, c0), rows[t], n1_l, c0, c1)
-                turn_fetched(y_sum, t, got, c0, c1)
-            if t == 2:
-                gated(0)
-                gated(1)
-        for n in range(4):
-            if n >= 2:
-                gated(n)
+        gated(0)
+        gated(1)
+        turn_back(0)
+        turn_back(1)
+        for n in (2, 3):
+            gated(n)
             turn_back(n)
 
-        pieces = [(0, 256), (256, 384), (384, 512)]
         z_c = sb("z_c", [P, S], U32)
         z_s = sb("z_s", [P, S], U8)
-        for c0, c1 in pieces:
+        for c0, c1 in Z_PIECES:
             z_g = sb("z_g%d" % c0, [P, PACK * (c1 - c0)], BF16)
             for jb in range(c0 // P, c1 // P):
                 nc.scalar.copy(
@@ -229,19 +222,20 @@ def tile_picked_twctriebpolar_none_p_kernel(
             quantize(z_c, z_s, z_g[:], c0, c1)
 
         s_sb = [sb("s_sb%d" % t, [P, S], F32) for t in range(PACK)]
+        last0, last1 = Z_PIECES[-1]
         acc = bank("a0", "s_acc0")
         last = bank("a1", "s_last")
-        for c0, c1 in pieces[:2]:
+        for c0, c1 in Z_PIECES[:-1]:
             product(acc, cw, cs, 0, z_c, z_s, c0, c1)
-        nc.scalar.activation(s_sb[0][:, 0:384], acc[:, 0:384], ACT.Copy, scale=0.0625)
-        product(last, cw, cs, 0, z_c, z_s, 384, 512)
-        nc.scalar.activation(s_sb[0][:, 384:512], last[:, 384:512], ACT.Copy, scale=0.0625)
-        cs_rest = deal("cs_rest", cand_s, U8, 1, PACK, "z_g256")
-        cw_rest = deal("cw_rest", cand_w, U32, 1, PACK, "z_g384")
+        nc.scalar.activation(s_sb[0][:, 0:last0], acc[:, 0:last0], ACT.Copy, scale=SCORE_SCALE)
+        product(last, cw, cs, 0, z_c, z_s, last0, last1)
+        nc.scalar.activation(s_sb[0][:, last0:last1], last[:, last0:last1], ACT.Copy, scale=SCORE_SCALE)
+        cs_rest = deal("cs_rest", cand_s, U8, 1, PACK, "z_g%d" % Z_PIECES[-2][0])
+        cw_rest = deal("cw_rest", cand_w, U32, 1, PACK, "z_g%d" % last0)
         for t in range(1, PACK):
             acc = bank(["a2", "a3", "b0"][t - 1], "s_acc%d" % t)
             product(acc, cw_rest, cs_rest, t - 1, z_c, z_s, 0, S)
-            nc.scalar.activation(s_sb[t][:], acc[:], ACT.Copy, scale=0.0625)
+            nc.scalar.activation(s_sb[t][:], acc[:], ACT.Copy, scale=SCORE_SCALE)
 
         out_rows = out.rearrange("(p t) s -> t p s", t=PACK)
         half_a, pb, ra, res = {}, {}, {}, {}

@@ -21,6 +21,7 @@ PACK = 4
 HALF = 256
 PER_COLUMN = 16
 SCORE_SCALE = 0.0625
+BANK_ORDER = (0, 2, 1, 3)
 Z_PIECES = [(0, 256), (256, 384), (384, 512)]
 
 
@@ -157,9 +158,6 @@ def tile_picked_twctriebpolar_none_p_kernel(
         def paired(bank_tile):
             return bank_tile[:].rearrange("j (i e p) -> j i p e", i=2, e=2)
 
-        def as_pairs(ap):
-            return ap.rearrange("j (i p e) -> j i p e", i=2, e=2)
-
         d_sum = [bank("b%d" % n, "d_sum%d" % n) for n in range(PACK)]
         y_rows, y_acc = [], []
         for t in range(PACK):
@@ -179,8 +177,8 @@ def tile_picked_twctriebpolar_none_p_kernel(
             nc.scalar.activation(y_rows[t][:, 0:S], y_acc[t][:], ACT.Copy, scale=gs_t[:, t : t + 1])
 
         gates = sb("gates", [P, PACK * H], F32, "gs_t")
-        gate = [as_pairs(gates[:, n * H : (n + 1) * H]) for n in range(PACK)]
-        for n in range(PACK):
+        gate = [gates[:, n * H : (n + 1) * H].rearrange("j (i p e) -> j i p e", i=2, e=2) for n in range(PACK)]
+        for n in BANK_ORDER:
             nc.scalar.activation(gate[n], paired(d_sum[n]), ACT.Sigmoid)
 
         y_sum = [bank("a%d" % n, "y_sum%d" % n) for n in range(PACK)]
@@ -191,24 +189,19 @@ def tile_picked_twctriebpolar_none_p_kernel(
                 fetch(got[:], y_rows[t], n1_l, c0, c1)
                 turn_fetched(y_sum, t, got, c0, c1)
 
-        z_first = sb("z_first", [P, 2 * H], BF16, "w1_g")
-        z_t = [z_first[:, 0:H], z_first[:, H : 2 * H]] + [sb("z_t%d" % n, [P, H], BF16)[:] for n in (2, 3)]
         z_w = [bank("b%d" % jb, "z_w%d" % jb) for jb in range(PACK)]
-
-        def gated(n):
-            nc.vector.tensor_tensor(as_pairs(z_t[n]), paired(y_sum[n]), gate[n], ALU.mult)
-
-        def turn_back(n):
-            for i in range(2):
-                nc.tensor.transpose(z_w[2 * (n % 2) + i][:, blk(n // 2)], z_t[n].bitcast(F32)[:, blk(i)], ident[:])
-
-        gated(0)
-        gated(1)
-        turn_back(0)
-        turn_back(1)
-        for n in (2, 3):
-            gated(n)
-            turn_back(n)
+        z_tags = {0: "w1_g", 1: "y_rows3"}
+        for n in BANK_ORDER:
+            for i0, i1 in [(0, 2)] if n != BANK_ORDER[-1] else [(0, 1), (1, 2)]:
+                z_t = sb("z_t%d_%d" % (n, i0), [P, (i1 - i0) * 2 * P], BF16, z_tags.get(n))
+                nc.vector.tensor_tensor(
+                    z_t[:].rearrange("j (i p e) -> j i p e", p=P, e=2),
+                    paired(y_sum[n])[:, i0:i1],
+                    gate[n][:, i0:i1],
+                    ALU.mult,
+                )
+                for i in range(i0, i1):
+                    nc.tensor.transpose(z_w[2 * (n % 2) + i][:, blk(n // 2)], z_t[:].bitcast(F32)[:, blk(i - i0)], ident[:])
 
         z_c = sb("z_c", [P, S], U32)
         z_s = sb("z_s", [P, S], U8)
@@ -222,18 +215,14 @@ def tile_picked_twctriebpolar_none_p_kernel(
             quantize(z_c, z_s, z_g[:], c0, c1)
 
         s_sb = [sb("s_sb%d" % t, [P, S], F32) for t in range(PACK)]
-        last0, last1 = Z_PIECES[-1]
-        acc = bank("a0", "s_acc0")
-        last = bank("a1", "s_last")
-        for c0, c1 in Z_PIECES[:-1]:
+        for n, (c0, c1) in enumerate(Z_PIECES):
+            acc = bank("a%d" % n, "s_piece%d" % n)
             product(acc, cw, cs, 0, z_c, z_s, c0, c1)
-        nc.scalar.activation(s_sb[0][:, 0:last0], acc[:, 0:last0], ACT.Copy, scale=SCORE_SCALE)
-        product(last, cw, cs, 0, z_c, z_s, last0, last1)
-        nc.scalar.activation(s_sb[0][:, last0:last1], last[:, last0:last1], ACT.Copy, scale=SCORE_SCALE)
+            nc.scalar.activation(s_sb[0][:, c0:c1], acc[:, c0:c1], ACT.Copy, scale=SCORE_SCALE)
         cs_rest = deal("cs_rest", cand_s, U8, 1, PACK, "z_g%d" % Z_PIECES[-2][0])
-        cw_rest = deal("cw_rest", cand_w, U32, 1, PACK, "z_g%d" % last0)
+        cw_rest = deal("cw_rest", cand_w, U32, 1, PACK, "z_g%d" % Z_PIECES[-1][0])
         for t in range(1, PACK):
-            acc = bank(["a2", "a3", "b0"][t - 1], "s_acc%d" % t)
+            acc = bank(["a3", "b0", "a0"][t - 1], "s_acc%d" % t)
             product(acc, cw_rest, cs_rest, t - 1, z_c, z_s, 0, S)
             nc.scalar.activation(s_sb[t][:], acc[:], ACT.Copy, scale=SCORE_SCALE)
 
@@ -260,7 +249,7 @@ def tile_picked_twctriebpolar_none_p_kernel(
             nc.scalar.activation(ra[t][:], total[:, 0:W], ACT.Sqrt, bias=0.25)
 
         def put_rb(t):
-            res[t] = sb("res%d" % t, [P, S], F32)
+            res[t] = sb("res%d" % t, [P, S], F32, "z_g%d" % Z_PIECES[-1][0] if t == 0 else None)
             nc.vector.tensor_tensor(res[t][:].indirect(n4_l[:]), pb[t][:], half_a[t][:], ALU.add)
 
         def put_ra(t):

from contextlib import ExitStack

import concourse.mybir as mybir
from concourse.masks import make_identity

T, S, H, C, W = 2048, 512, 512, 512, 256
FLOPS = 3 * 2 * 512 * 512 * 512

F32 = mybir.dt.float32
BF16 = mybir.dt.bfloat16
I32 = mybir.dt.int32
U32 = mybir.dt.uint32
U16 = mybir.dt.uint16
U8 = mybir.dt.uint8
FP8X4 = mybir.dt.float8_e4m3fn_x4
ACT = mybir.ActivationFunctionType
ALU = mybir.AluOpType

P = 128
PACK = 4
HALF = 256
PER_COLUMN = 16
SCORE_SCALE = 0.0625
BANK_ORDER = (0, 2, 1, 3)
Z_PIECES = [(0, 256), (256, 384), (384, 512)]


def tile_picked_twctriebpolar_none_p_kernel(
    tc, x_words, x_scales, w1, w2, gs, offs, two, n1, n2, cand, n3, n4, out
):
    nc = tc.nc
    with ExitStack() as ctx:
        keep = ctx.enter_context(tc.tile_pool(name="keep", bufs=1))
        psum = ctx.enter_context(tc.psum_pool(name="psum", bufs=1))

        def sb(name, shape, dtype, tag=None):
            return keep.tile(shape, dtype, name=name, tag=tag or name, align_bytes=64)

        def bank(tag, name):
            return psum.tile([P, 512], F32, name=name, tag=tag)

        def blk(i):
            return slice(i * P, (i + 1) * P)

        def load_list(name, src):
            tile = keep.tile(list(src.shape), U16, name=name)
            nc.sync.dma_start(tile[:], src)
            return tile

        def load_weight_half(name, w, h):
            raw = sb(name, [P, PACK * HALF], F32)
            nc.sync.dma_start(
                raw[:].rearrange("p (j c) -> p j c", j=PACK),
                w.rearrange("(p j) c -> p j c", j=PACK)[:, :, h * HALF : (h + 1) * HALF],
            )
            return raw

        def cast_weight_half(grouped, raw, h):
            m = HALF // PACK
            nc.scalar.copy(
                grouped[:].rearrange("p (t m j) -> p m j t", t=PACK, j=PACK)[:, h * m : (h + 1) * m],
                raw[:].rearrange("p (j m t) -> p m j t", j=PACK, t=PACK),
            )

        def gather_packed(picked, table, offsets):
            nc.vector.tensor_copy(picked, table.indirect(offsets[:]))
            return picked

        def deal(name, picked, dtype, t0, t1, tag=None):
            dealt = sb(name, [P, (t1 - t0) * P], dtype, tag)
            nc.vector.tensor_copy(
                dealt[:].rearrange("p (t m) -> p m t", m=P), picked.rearrange("p (m t) -> p m t", t=PACK)[:, :, t0:t1]
            )
            return dealt

        def quantize(codes, scales, src, c0, c1):
            nc.vector.quantize_mx(out=codes[:, c0:c1].bitcast(FP8X4), scales=scales[:, c0:c1], in_=src)

        def product(acc, l_codes, l_scales, t, r_codes, r_scales, c0, c1):
            nc.tensor.matmul_mx(
                out=acc[:, c0:c1],
                lhsT=l_codes[:, blk(t)].bitcast(FP8X4),
                lhsT_scale=l_scales[:, blk(t)],
                rhs=r_codes[:, c0:c1].bitcast(FP8X4),
                rhs_scale=r_scales[:, c0:c1],
                start=True,
                stop=True,
            )

        def turn(dst, src, start, stop):
            nc.tensor.matmul(dst, lhsT=src, rhs=ident[:], is_transpose=True, start=start, stop=stop)

        def fetch(got, window, offsets, c0, c1):
            nc.vector.tensor_copy(got, window[:].indirect(offsets[:, c0 // PER_COLUMN : c1 // PER_COLUMN]))

        xs = sb("xs", [P, T], U8)
        nc.gpsimd.memset(xs[:].bitcast(I32), 0)
        two_l = load_list("two_l", two)
        offs_l = load_list("offs_l", offs)
        cand_l = load_list("cand_l", cand)
        for q in range(4):
            nc.sync.dma_start(xs[32 * q : 32 * q + 4, :].bitcast(I32), x_scales[0, 4 * q : 4 * q + 4, :].bitcast(I32))
        xw = sb("xw", [P, T], I32)
        nc.sync.dma_start(xw[:], x_words[0].rearrange("p n t -> p (n t)").bitcast(I32))
        w2_raw = [load_weight_half("w2_raw%d" % h, w2, h) for h in range(2)]
        w1_raw = [load_weight_half("w1_raw%d" % h, w1, h) for h in range(2)]
        n2_l = load_list("n2_l", n2)
        gs_t = sb("gs_t", [P, PACK], F32)
        nc.sync.dma_start(gs_t[:], gs.rearrange("(p t) o -> p (t o)", t=PACK))
        n1_l = load_list("n1_l", n1)
        n3_l = load_list("n3_l", n3)
        n4_l = load_list("n4_l", n4)

        ident = sb("ident", [P, P], F32)
        make_identity(nc, ident[:])

        words = xw[:].bitcast(U32)
        picked_s = sb("picked_s", [P, 3 * S], U8)
        two_s, offs_s, cand_s = [
            gather_packed(picked_s[:, n * S : (n + 1) * S], xs[:], lst) for n, lst in enumerate((two_l, offs_l, cand_l))
        ]
        two_w = gather_packed(sb("two_w", [P, S], U32)[:], words, two_l)
        offs_w = gather_packed(sb("offs_w", [P, S], U32)[:], words, offs_l)

        w2_g = sb("w2_g", [P, PACK * H], BF16)
        for h in range(2):
            cast_weight_half(w2_g, w2_raw[h], h)
        w2_c = sb("w2_c", [P, H], U32)
        w2_s = sb("w2_s", [P, H], U8)
        quantize(w2_c, w2_s, w2_g[:], 0, H)

        cand_w = gather_packed(sb("cand_w", [P, C], U32, "w2_g")[:], words, cand_l)
        cs = deal("cs", cand_s, U8, 0, 1)
        cw = deal("cw", cand_w, U32, 0, 1)

        w1_g = sb("w1_g", [P, PACK * H], BF16)
        cast_weight_half(w1_g, w1_raw[0], 0)
        d_rows = [w2_raw[0], w2_raw[1], w1_raw[1], w1_raw[0]]
        for t in range(PACK):
            acc = bank("a%d" % t, "d_acc%d" % t)
            product(acc, w2_c, w2_s, t, two_w, two_s, 0, S)
            nc.scalar.copy(d_rows[t][:, 0:S], acc[:])
            if t == 1:
                cast_weight_half(w1_g, w1_raw[1], 1)

        def place(sums, t, jb):
            c0 = (jb % 2) * 2 * P + (t % 2) * P
            return sums[2 * (t // 2) + jb // 2][:, c0 : c0 + P]

        def turn_own(sums, t, own):
            for jb in range(PACK):
                turn(place(sums, t, jb), own[:, blk(jb)], t % 2 == 0 and jb % 2 == 0, False)

        def turn_fetched(sums, t, got, c0, c1):
            for jb in range(c0 // P, c1 // P):
                turn(place(sums, t, jb), got[:, blk(jb - c0 // P)], False, t % 2 == 1 and jb % 2 == 1)

        def paired(bank_tile):
            return bank_tile[:].rearrange("j (i e p) -> j i p e", i=2, e=2)

        d_sum = [bank("b%d" % n, "d_sum%d" % n) for n in range(PACK)]
        y_rows, y_acc = [], []
        for t in range(PACK):
            turn_own(d_sum, t, d_rows[t])
            y_rows.append(sb("y_rows%d" % t, [P, 2 * S], F32, "w1_g" if t == 2 else None))
            fetch(y_rows[t][:, S : 2 * S], d_rows[t], n2_l, 0, S)
            turn_fetched(d_sum, t, y_rows[t][:, S : 2 * S], 0, S)
            if t == 1:
                w1_c = sb("w1_c", [P, H], U32)
                w1_s = sb("w1_s", [P, H], U8)
                quantize(w1_c, w1_s, w1_g[:], 0, H)
                for n in range(PACK):
                    y_acc.append(bank("a%d" % n, "y_acc%d" % n))
                    product(y_acc[n], w1_c, w1_s, n, offs_w, offs_s, 0, S)

        for t in range(PACK):
            nc.scalar.activation(y_rows[t][:, 0:S], y_acc[t][:], ACT.Copy, scale=gs_t[:, t : t + 1])

        gates = sb("gates", [P, PACK * H], F32, "gs_t")
        gate = [gates[:, n * H : (n + 1) * H].rearrange("j (i p e) -> j i p e", i=2, e=2) for n in range(PACK)]
        for n in BANK_ORDER:
            nc.scalar.activation(gate[n], paired(d_sum[n]), ACT.Sigmoid)

        y_sum = [bank("a%d" % n, "y_sum%d" % n) for n in range(PACK)]
        for t in range(PACK):
            turn_own(y_sum, t, y_rows[t])
            for c0, c1 in [(0, S)] if t < PACK - 1 else [(0, HALF), (HALF, S)]:
                got = sb("y_got%d_%d" % (t, c0), [P, c1 - c0], F32)
                fetch(got[:], y_rows[t], n1_l, c0, c1)
                turn_fetched(y_sum, t, got, c0, c1)

        z_w = [bank("b%d" % jb, "z_w%d" % jb) for jb in range(PACK)]
        z_tags = {0: "w1_g", 1: "y_rows3"}
        for n in BANK_ORDER:
            for i0, i1 in [(0, 2)] if n != BANK_ORDER[-1] else [(0, 1), (1, 2)]:
                z_t = sb("z_t%d_%d" % (n, i0), [P, (i1 - i0) * 2 * P], BF16, z_tags.get(n))
                nc.vector.tensor_tensor(
                    z_t[:].rearrange("j (i p e) -> j i p e", p=P, e=2),
                    paired(y_sum[n])[:, i0:i1],
                    gate[n][:, i0:i1],
                    ALU.mult,
                )
                for i in range(i0, i1):
                    nc.tensor.transpose(z_w[2 * (n % 2) + i][:, blk(n // 2)], z_t[:].bitcast(F32)[:, blk(i - i0)], ident[:])

        z_c = sb("z_c", [P, S], U32)
        z_s = sb("z_s", [P, S], U8)
        for c0, c1 in Z_PIECES:
            z_g = sb("z_g%d" % c0, [P, PACK * (c1 - c0)], BF16)
            for jb in range(c0 // P, c1 // P):
                nc.scalar.copy(
                    z_g[:].bitcast(F32)[:, 2 * (P * jb - c0) : 2 * (P * (jb + 1) - c0)].rearrange("p (j u) -> p j u", u=2),
                    z_w[jb][:, 0 : 2 * P].rearrange("p (u j) -> p j u", u=2),
                )
            quantize(z_c, z_s, z_g[:], c0, c1)

        s_sb = [sb("s_sb%d" % t, [P, S], F32) for t in range(PACK)]
        for n, (c0, c1) in enumerate(Z_PIECES):
            acc = bank("a%d" % n, "s_piece%d" % n)
            product(acc, cw, cs, 0, z_c, z_s, c0, c1)
            nc.scalar.activation(s_sb[0][:, c0:c1], acc[:, c0:c1], ACT.Copy, scale=SCORE_SCALE)
        cs_rest = deal("cs_rest", cand_s, U8, 1, PACK, "z_g%d" % Z_PIECES[-2][0])
        cw_rest = deal("cw_rest", cand_w, U32, 1, PACK, "z_g%d" % Z_PIECES[-1][0])
        for t in range(1, PACK):
            acc = bank(["a3", "b0", "a0"][t - 1], "s_acc%d" % t)
            product(acc, cw_rest, cs_rest, t - 1, z_c, z_s, 0, S)
            nc.scalar.activation(s_sb[t][:], acc[:], ACT.Copy, scale=SCORE_SCALE)

        out_rows = out.rearrange("(p t) s -> t p s", t=PACK)
        half_a, pb, ra, res = {}, {}, {}, {}

        def pairs(t):
            half_a[t] = sb("half_a%d" % t, [P, W], F32)
            pb[t] = sb("pb%d" % t, [P, W], F32)
            nc.vector.tensor_scalar(half_a[t][:], s_sb[t][:].indirect(n3_l[:]), -0.5, 0.0, ALU.mult, ALU.add)
            nc.vector.tensor_copy(pb[t][:], s_sb[t][:].indirect(n4_l[:]))
            turned = bank(["b1", "b3"][t % 2], "turned%d" % t)
            for i in range(2):
                nc.tensor.transpose(turned[:, blk(i)], half_a[t][:, blk(i)], ident[:])
                nc.tensor.transpose(turned[:, blk(2 + i)], pb[t][:, blk(i)], ident[:])
            sq = sb("sq%d" % t, [P, 2 * W], F32)
            nc.scalar.activation(sq[:, 0:W], turned[:, 0:W], ACT.Square, scale=2.0)
            nc.scalar.activation(sq[:, W : 2 * W], turned[:, W : 2 * W], ACT.Square)
            total = bank(["b2", "a1"][t % 2], "total%d" % t)
            for i in range(2):
                turn(total[:, blk(i)], sq[:, blk(i)], True, False)
                turn(total[:, blk(i)], sq[:, blk(2 + i)], False, True)
            ra[t] = sb("ra%d" % t, [P, W], F32)
            nc.scalar.activation(ra[t][:], total[:, 0:W], ACT.Sqrt, bias=0.25)

        def put_rb(t):
            res[t] = sb("res%d" % t, [P, S], F32, "z_g%d" % Z_PIECES[-1][0] if t == 0 else None)
            nc.vector.tensor_tensor(res[t][:].indirect(n4_l[:]), pb[t][:], half_a[t][:], ALU.add)

        def put_ra(t):
            nc.vector.tensor_copy(res[t][:].indirect(n3_l[:]), ra[t][:])
            nc.sync.dma_start(out_rows[t], res[t][:])

        pairs(0)
        pairs(1)
        put_rb(0)
        put_rb(1)
        put_ra(0)
        pairs(2)
        put_ra(1)
        pairs(3)
        put_rb(2)
        put_rb(3)
        put_ra(2)
        put_ra(3)
